import numpy as np, ml_dtypes
CORES = [32,160,288,416,80,208,336,464]
N = 8
import mx_ref
NC, G, MB = 128, 2, 3
C = np.float32(0.023)
BF = ml_dtypes.bfloat16
def cut(t, i, w=512):
    return t[:, w * i:w * i + w]
def tile(rs):
    return np.stack(rs, axis=2).reshape(128, -1).astype(BF)
def layer(w, X):
    out = []
    for i in range(G):
        for t in range(len(X)):
            p = mx_ref.matmul(mx_ref.quantize(cut(w, len(X) * i + t)), X[t])
            z = p if t == 0 else z + p
        out.append(z)
    return out
def act(Z):
    return [np.maximum(s * z, 0) * C for z in Z for s in (1, -1)]
def setup_inputs(rng):
    def f(*shape):
        return mx_ref.flush((rng.standard_normal(shape, dtype=np.float32) * np.exp2(rng.integers(-2, 3, shape[:-1] + (1,)))).astype(BF))
    return {"x": f(N, 128, MB * 4 * NC), "w": f(N, 128, G * 512)}
def setup_inputs_blocks(rng):
    d = setup_inputs(rng)
    for k in ("x",): d[k] = mx_ref.spread(d[k], rng, 4)
    for k in ("w",): d[k] = mx_ref.spread(d[k], rng, 1)
    return d
def setup_inputs_wide(rng):
    d = setup_inputs(rng)
    for k in ("x",): d[k] = mx_ref.flush((d[k].astype(np.float32) * np.exp2(rng.integers(-8, 9, (N, 1, 1))).astype(np.float32)).astype(BF))
    return d
def setup_inputs_zeros(rng):
    d = setup_inputs(rng); v = d["x"].reshape(N, 128, -1, 4).copy()
    v[np.broadcast_to((rng.random((N, 1, v.shape[2], 1)) < 0.33), v.shape)] = 0
    d["x"] = v.reshape(d["x"].shape)
    return d
def reference(x, w):
    y = np.full((N, 128, MB * G * NC), np.nan, np.float32)
    for m in range(MB):
        a = mx_ref.quantize(cut(x[N - 1], m, 4 * NC))
        for s in range(N - 1):
            a = mx_ref.quantize(tile(act(layer(w[s], [a]))))
        Z = layer(w[N - 1], [a])
        for i in range(G):
            y[N - 1][:, NC * (G * m + i):NC * (G * m + i) + NC] = Z[i]
    return {"y": y}

@@ -1,0 +1,124 @@
+import numpy as np
+from concourse.mybir import dt, AluOpType, ActivationFunctionType
+
+N = 8
+COLS = 384
+TILE = 128
+CONST = float(np.float32(0.023))
+
+_P = [(0, 128), (128, 256), (256, 384)]
+PLAN = [_P] * N
+MAXP = 3
+
+SCRATCH = {
+    "wt":   ("sbuf", [128, 1024], "bfloat16"),
+    "wq":   ("sbuf", [128, 256], "float8_e4m3fn_x4"),
+    "wsc":  ("sbuf", [128, 256], "uint8"),
+    "tl":   ("sbuf", [128, 4 * COLS], "bfloat16"),
+    "outq": ("sbuf", [128, COLS], "float8_e4m3fn_x4"),
+    "outs": ("sbuf", [128, COLS], "uint8"),
+    "inq":  ("sbuf", [128, COLS], "float8_e4m3fn_x4"),
+    "ins":  ("sbuf", [128, COLS], "uint8"),
+    "ps":   ("psum", [128, 512 * 2 * MAXP], "float32"),
+    "yb":   ("sbuf", [128, 2 * COLS], "float32"),
+}
+SEMAPHORES = (["wl", "wqd", "sent", "stored"]
+              + ["%s%d" % (n, j) for n in ("xl", "arr", "za", "zb", "act", "qd", "ca", "cb") for j in range(MAXP)])
+
+
+def rank_program(g, core, T, topo):
+    rank = T.rank_of(core)
+    if rank is None:
+        return
+    S = T.sem
+    last = rank == N - 1
+    out_plan = PLAN[rank]
+    in_plan = PLAN[(rank - 1) % N]
+    comp_plan = in_plan if last else out_plan
+
+    def engines(src, dst):
+        m = topo.mask(src, dst)
+        e = [i for i in range(m.bit_length()) if (m >> i) & 1]
+        return e[0::2], e[1::2]
+
+    def bits(e):
+        return sum(1 << i for i in e)
+
+    if last:
+        for j, (a, b) in enumerate(out_plan):
+            g.sync.dma_start(T.tl[:, 4 * a:4 * b], T.x[:, 4 * a:4 * b]).then_inc(S["xl%d" % j], 16)
+    g.sync.dma_start(T.wt[:, :], T.w[:, :]).then_inc(S.wl, 16)
+
+    if last:
+        for j, (a, b) in enumerate(out_plan):
+            g.vector.wait_ge(S["xl%d" % j], 16)
+            g.vector.quantize_mx(T.outq[:, a:b], T.outs[:, a:b], T.tl[:, 4 * a:4 * b]).then_inc(S["qd%d" % j], 1)
+    g.vector.wait_ge(S.wl, 16)
+    g.vector.quantize_mx(T.wq[:, :], T.wsc[:, :], T.wt[:, :]).then_inc(S.wqd, 1)
+
+    src = T.cores[(rank - 1) % N]
+    ec, es = engines(src, core)
+    arrive = len(ec) + len(es)
+    g.tensor.wait_ge(S.wqd, 1)
+    seen = 0
+    for j, (a, b) in enumerate(comp_plan):
+        while seen < len(in_plan) and in_plan[seen][0] < b:
+            g.tensor.wait_ge(S["arr%d" % seen], arrive)
+            seen += 1
+        for i, z in enumerate(("za", "zb")):
+            k = 512 * (2 * j + i)
+            g.tensor.matmul_mx(T.ps[:, k:k + b - a], T.wq[:, 128 * i:128 * i + 128], T.wsc[:, 128 * i:128 * i + 128],
+                               T.inq[:, a:b], T.ins[:, a:b], True, True).then_inc(S["%s%d" % (z, j)], 1)
+
+    if not last:
+        for j, (a, b) in enumerate(comp_plan):
+            za = T.ps[:, 512 * 2 * j:512 * 2 * j + b - a]
+            zb = T.ps[:, 512 * (2 * j + 1):512 * (2 * j + 1) + b - a]
+            act = S["act%d" % j]
+            g.vector.wait_ge(S["za%d" % j], 1)
+            g.vector.tensor_scalar(T.tl[:, 4 * a + 0:4 * b:4], za, 0.0, CONST, AluOpType.max, AluOpType.mult).then_inc(act, 1)
+            g.vector.tensor_scalar(T.tl[:, 4 * a + 1:4 * b:4], za, -CONST, 0.0, AluOpType.mult, AluOpType.max).then_inc(act, 1)
+            g.scalar.wait_ge(S["zb%d" % j], 1)
+            g.scalar.activation(T.tl[:, 4 * a + 2:4 * b:4], zb, ActivationFunctionType.Relu, scale=CONST).then_inc(act, 1)
+            g.scalar.activation(T.tl[:, 4 * a + 3:4 * b:4], zb, ActivationFunctionType.Relu, scale=-CONST).then_inc(act, 1)
+            g.vector.wait_ge(act, 4)
+            g.vector.quantize_mx(T.outq[:, a:b], T.outs[:, a:b], T.tl[:, 4 * a:4 * b]).then_inc(S["qd%d" % j], 1)
+
+    dst = T.cores[(rank + 1) % N]
+    rid, pid = topo.addr(dst, core)
+    ec, es = engines(core, dst)
+    left = 0
+    for j, (a, b) in enumerate(out_plan):
+        g.wait_ge(S["qd%d" % j], 1)
+        g.remote_dma(T.inq[:, a:b].bitcast(dt.uint8), T.outq[:, a:b].bitcast(dt.uint8),
+                     S["arr%d" % j], S.sent, pid, rid, bits(ec))
+        g.remote_dma(T.ins[:, a:b], T.outs[:, a:b], S["arr%d" % j], S.sent, pid, rid, bits(es))
+        left += len(ec) + len(es)
+
+    if last:
+        stores = 0
+        for j, (a, b) in enumerate(comp_plan):
+            cuts = []
+            for m in range(a // TILE, (b + TILE - 1) // TILE):
+                cuts.append((m, max(a, m * TILE), min(b, (m + 1) * TILE)))
+            g.vector.wait_ge(S["za%d" % j], 1)
+            g.scalar.wait_ge(S["zb%d" % j], 1)
+            for i in range(2):
+                for (m, lo, hi) in cuts:
+                    k = 512 * (2 * j + i)
+                    z = T.ps[:, k + lo - a:k + hi - a]
+                    o = TILE * (2 * m + i) - m * TILE
+                    if i == 0:
+                        g.vector.tensor_copy(T.yb[:, o + lo:o + hi], z).then_inc(S["ca%d" % j], 1)
+                    else:
+                        g.scalar.activation(T.yb[:, o + lo:o + hi], z, ActivationFunctionType.Copy).then_inc(S["cb%d" % j], 1)
+            g.sync.wait_ge(S["ca%d" % j], len(cuts))
+            g.scalar.wait_ge(S["cb%d" % j], len(cuts))
+            for i, q in enumerate((g.sync, g.scalar)):
+                for (m, lo, hi) in cuts:
+                    o = TILE * (2 * m + i) - m * TILE
+                    q.dma_start(T.y[:, o + lo:o + hi], T.yb[:, o + lo:o + hi]).then_inc(S.stored, 16)
+                    stores += 1
+        g.wait_ge(S.stored, 16 * stores)
+
+    g.wait_ge(S.sent, left)

@@ -2,123 +2,187 @@ import numpy as np
 from concourse.mybir import dt, AluOpType, ActivationFunctionType
 
 N = 8
+WORLD = 512
 COLS = 384
 TILE = 128
+HW = 192
+HALVES = [(0, HW), (HW, COLS)]
 CONST = float(np.float32(0.023))
 
-_P = [(0, 128), (128, 256), (256, 384)]
-PLAN = [_P] * N
-MAXP = 3
+SEQ = [[(0, (0,)), (1, (1, 2)), (4, (3, 4)), (5, (5, 6)), (N - 1, (N - 1,))],
+       [(0, (0,)), (2, (1, 2)), (3, (3, 4)), (6, (5, 6)), (N - 1, (N - 1,))]]
 
 SCRATCH = {
-    "wt":   ("sbuf", [128, 1024], "bfloat16"),
-    "wq":   ("sbuf", [128, 256], "float8_e4m3fn_x4"),
-    "wsc":  ("sbuf", [128, 256], "uint8"),
-    "tl":   ("sbuf", [128, 4 * COLS], "bfloat16"),
-    "outq": ("sbuf", [128, COLS], "float8_e4m3fn_x4"),
-    "outs": ("sbuf", [128, COLS], "uint8"),
-    "inq":  ("sbuf", [128, COLS], "float8_e4m3fn_x4"),
-    "ins":  ("sbuf", [128, COLS], "uint8"),
-    "ps":   ("psum", [128, 512 * 2 * MAXP], "float32"),
-    "yb":   ("sbuf", [128, 2 * COLS], "float32"),
+    "wt":  ("sbuf", [128, 1024], "bfloat16"),
+    "wq":  ("sbuf", [128, 256], "float8_e4m3fn_x4"),
+    "wsc": ("sbuf", [128, 256], "uint8"),
+    "fq":  ("sbuf", [128, 256], "float8_e4m3fn_x4"),
+    "fsc": ("sbuf", [128, 256], "uint8"),
+    "xt":  ("sbuf", [128, 4 * COLS], "bfloat16"),
+    "xq":  ("sbuf", [128, COLS], "float8_e4m3fn_x4"),
+    "xsc": ("sbuf", [128, COLS], "uint8"),
+    "tl":  ("sbuf", [128, 4 * 2 * HW], "bfloat16"),
+    "oq":  ("sbuf", [128, 2 * HW], "float8_e4m3fn_x4"),
+    "osc": ("sbuf", [128, 2 * HW], "uint8"),
+    "inq": ("sbuf", [128, COLS], "float8_e4m3fn_x4"),
+    "ins": ("sbuf", [128, COLS], "uint8"),
+    "ps":  ("psum", [128, 512 * 4], "float32"),
+    "yb":  ("sbuf", [128, 2 * COLS], "float32"),
 }
-SEMAPHORES = (["wl", "wqd", "sent", "stored"]
-              + ["%s%d" % (n, j) for n in ("xl", "arr", "za", "zb", "act", "qd", "ca", "cb") for j in range(MAXP)])
+SEMAPHORES = (["wl", "wqd", "warr", "sent", "stored"]
+              + ["%s%d" % (n, j) for n in ("xl", "xqd", "arr", "za", "zb", "act", "qd", "ca", "cb") for j in range(2)])
+
+_CACHE = {}
+
+
+def _roads(T, topo):
+    if "r" in _CACHE:
+        return _CACHE["r"]
+    cores = list(T.cores)
+
+    def place(c):
+        return (topo.host(c), topo.chip(c))
+
+    def one_link(a, b):
+        if topo.rack(topo.host(a)) != topo.rack(topo.host(b)):
+            return topo.chip(a) == topo.chip(b)
+        return topo.same_plane(a, b)
+
+    full = [[(cores[N - 1], "x")] + [(cores[r], st) for r, st in seq] for seq in SEQ]
+    roads = []
+    for h, seq in enumerate(full):
+        other = full[1 - h]
+        road = [seq[0]]
+        for k in range(1, len(seq)):
+            a, b = seq[k - 1][0], seq[k][0]
+            if not topo.may_write(a, b):
+                shun = (place(other[k - 1][0]), place(other[k][0]))
+                road.append(([c for c in range(WORLD) if c not in cores and topo.may_write(a, c) and topo.may_write(c, b)
+                              and one_link(a, c) and one_link(c, b) and topo.die(c) == topo.die(a)
+                              and place(c) not in shun][0], ()))
+            road.append(seq[k])
+        roads.append(road)
+    _CACHE["r"] = roads
+    return roads
 
 
 def rank_program(g, core, T, topo):
-    rank = T.rank_of(core)
-    if rank is None:
+    roads = _roads(T, topo)
+    jobs = [(h, k, st) for h, road in enumerate(roads) for k, (c, st) in enumerate(road) if c == core]
+    if not jobs:
         return
+    rank = T.rank_of(core)
     S = T.sem
     last = rank == N - 1
-    out_plan = PLAN[rank]
-    in_plan = PLAN[(rank - 1) % N]
-    comp_plan = in_plan if last else out_plan
+    left = [0]
 
     def engines(src, dst):
         m = topo.mask(src, dst)
         e = [i for i in range(m.bit_length()) if (m >> i) & 1]
         return e[0::2], e[1::2]
 
-    def bits(e):
-        return sum(1 << i for i in e)
+    def lands(src):
+        ec, es = engines(src, core)
+        return len(ec) + len(es)
+
+    def send(dst, dq, ds, sq, ss, sem):
+        rid, pid = topo.addr(dst, core)
+        ec, es = engines(core, dst)
+        g.remote_dma(dq.bitcast(dt.uint8), sq.bitcast(dt.uint8), sem, S.sent, pid, rid, sum(1 << i for i in ec))
+        g.remote_dma(ds, ss, sem, S.sent, pid, rid, sum(1 << i for i in es))
+        left[0] += len(ec) + len(es)
 
     if last:
-        for j, (a, b) in enumerate(out_plan):
-            g.sync.dma_start(T.tl[:, 4 * a:4 * b], T.x[:, 4 * a:4 * b]).then_inc(S["xl%d" % j], 16)
-    g.sync.dma_start(T.wt[:, :], T.w[:, :]).then_inc(S.wl, 16)
+        for h, (a, b) in enumerate(HALVES):
+            (g.sync, g.scalar)[h].dma_start(T.xt[:, 4 * a:4 * b], T.x[:, 4 * a:4 * b]).then_inc(S["xl%d" % h], 16)
+    if rank is not None:
+        g.sync.dma_start(T.wt[:, :], T.w[:, :]).then_inc(S.wl, 16)
+    if last:
+        for h, (a, b) in enumerate(HALVES):
+            g.vector.wait_ge(S["xl%d" % h], 16)
+            g.vector.quantize_mx(T.xq[:, a:b], T.xsc[:, a:b], T.xt[:, 4 * a:4 * b]).then_inc(S["xqd%d" % h], 1)
+    if rank is not None:
+        g.vector.wait_ge(S.wl, 16)
+        g.vector.quantize_mx(T.wq[:, :], T.wsc[:, :], T.wt[:, :]).then_inc(S.wqd, 1)
+        takers = [c for road in roads for (c, st) in road if st != "x" and rank in st and c != core]
+        if takers:
+            g.wait_ge(S.wqd, 1)
+        for c in takers:
+            send(c, T.fq[:, :], T.fsc[:, :], T.wq[:, :], T.wsc[:, :], S.warr)
+
+    slot = 0
+    ready = set()
+    ycols = []
+    for (h, k, st) in jobs:
+        a, b = HALVES[h]
+        road = roads[h]
+        arr = S["arr%d" % h]
+        if st == "x":
+            g.wait_ge(S["xqd%d" % h], 1)
+            send(road[k + 1][0], T.inq[:, a:b], T.ins[:, a:b], T.xq[:, a:b], T.xsc[:, a:b], arr)
+            continue
+        if st == ():
+            g.wait_ge(arr, lands(road[k - 1][0]))
+            send(road[k + 1][0], T.inq[:, a:b], T.ins[:, a:b], T.inq[:, a:b], T.ins[:, a:b], arr)
+            continue
+        cq, cs = T.inq[:, a:b], T.ins[:, a:b]
+        for t, s in enumerate(st):
+            if s == rank:
+                wq, ws, wsem, wn = T.wq, T.wsc, S.wqd, 1
+            else:
+                wq, ws, wsem, wn = T.fq, T.fsc, S.warr, lands(T.cores[s])
+            if s not in ready:
+                g.tensor.wait_ge(wsem, wn)
+                ready.add(s)
+            if t == 0:
+                g.tensor.wait_ge(arr, lands(road[k - 1][0]))
+            else:
+                g.tensor.wait_ge(S["qd%d" % (slot - 1)], 1)
+            z = []
+            for i, nm in enumerate(("za", "zb")):
+                o = 512 * (2 * slot + i)
+                z.append(T.ps[:, o:o + HW])
+                g.tensor.matmul_mx(z[i], wq[:, 128 * i:128 * i + 128], ws[:, 128 * i:128 * i + 128],
+                                   cq, cs, True, True).then_inc(S["%s%d" % (nm, slot)], 1)
+            g.vector.wait_ge(S["za%d" % slot], 1)
+            g.scalar.wait_ge(S["zb%d" % slot], 1)
+            if s < N - 1:
+                lo, hi = 4 * HW * slot, 4 * HW * (slot + 1)
+                act = S["act%d" % slot]
+                g.vector.tensor_scalar(T.tl[:, lo + 0:hi:4], z[0], 0.0, CONST, AluOpType.max, AluOpType.mult).then_inc(act, 1)
+                g.vector.tensor_scalar(T.tl[:, lo + 1:hi:4], z[0], -CONST, 0.0, AluOpType.mult, AluOpType.max).then_inc(act, 1)
+                g.scalar.activation(T.tl[:, lo + 2:hi:4], z[1], ActivationFunctionType.Relu, scale=CONST).then_inc(act, 1)
+                g.scalar.activation(T.tl[:, lo + 3:hi:4], z[1], ActivationFunctionType.Relu, scale=-CONST).then_inc(act, 1)
+                cq, cs = T.oq[:, HW * slot:HW * (slot + 1)], T.osc[:, HW * slot:HW * (slot + 1)]
+                g.vector.wait_ge(act, 4)
+                g.vector.quantize_mx(cq, cs, T.tl[:, lo:hi]).then_inc(S["qd%d" % slot], 1)
+            else:
+                filled = set()
+                for m in range(a // TILE, (b + TILE - 1) // TILE):
+                    lo, hi = max(a, m * TILE), min(b, (m + 1) * TILE)
+                    for i in range(2):
+                        o = TILE * (2 * m + i) - m * TILE
+                        zz = T.ps[:, 512 * (2 * slot + i) + lo - a:512 * (2 * slot + i) + hi - a]
+                        if i == 0:
+                            g.vector.tensor_copy(T.yb[:, o + lo:o + hi], zz).then_inc(S["ca%d" % h], 1)
+                        else:
+                            g.scalar.activation(T.yb[:, o + lo:o + hi], zz, ActivationFunctionType.Copy).then_inc(S["cb%d" % h], 1)
+                        filled.update(range(o + lo, o + hi))
+                ycols.append((h, filled, (b + TILE - 1) // TILE - a // TILE))
+            slot += 1
+        if k + 1 < len(road):
+            g.wait_ge(S["qd%d" % (slot - 1)], 1)
+            send(road[k + 1][0], T.inq[:, a:b], T.ins[:, a:b], cq, cs, arr)
 
     if last:
-        for j, (a, b) in enumerate(out_plan):
-            g.vector.wait_ge(S["xl%d" % j], 16)
-            g.vector.quantize_mx(T.outq[:, a:b], T.outs[:, a:b], T.tl[:, 4 * a:4 * b]).then_inc(S["qd%d" % j], 1)
-    g.vector.wait_ge(S.wl, 16)
-    g.vector.quantize_mx(T.wq[:, :], T.wsc[:, :], T.wt[:, :]).then_inc(S.wqd, 1)
+        cut = 0
+        while cut in ycols[0][1]:
+            cut += 1
+        for j, (lo, hi) in enumerate(((0, cut), (cut, 2 * COLS))):
+            h, _, n = ycols[j]
+            g.sync.wait_ge(S["ca%d" % h], n)
+            g.sync.wait_ge(S["cb%d" % h], n)
+            g.sync.dma_start(T.y[:, lo:hi], T.yb[:, lo:hi]).then_inc(S.stored, 16)
+        g.wait_ge(S.stored, 32)
 
-    src = T.cores[(rank - 1) % N]
-    ec, es = engines(src, core)
-    arrive = len(ec) + len(es)
-    g.tensor.wait_ge(S.wqd, 1)
-    seen = 0
-    for j, (a, b) in enumerate(comp_plan):
-        while seen < len(in_plan) and in_plan[seen][0] < b:
-            g.tensor.wait_ge(S["arr%d" % seen], arrive)
-            seen += 1
-        for i, z in enumerate(("za", "zb")):
-            k = 512 * (2 * j + i)
-            g.tensor.matmul_mx(T.ps[:, k:k + b - a], T.wq[:, 128 * i:128 * i + 128], T.wsc[:, 128 * i:128 * i + 128],
-                               T.inq[:, a:b], T.ins[:, a:b], True, True).then_inc(S["%s%d" % (z, j)], 1)
-
-    if not last:
-        for j, (a, b) in enumerate(comp_plan):
-            za = T.ps[:, 512 * 2 * j:512 * 2 * j + b - a]
-            zb = T.ps[:, 512 * (2 * j + 1):512 * (2 * j + 1) + b - a]
-            act = S["act%d" % j]
-            g.vector.wait_ge(S["za%d" % j], 1)
-            g.vector.tensor_scalar(T.tl[:, 4 * a + 0:4 * b:4], za, 0.0, CONST, AluOpType.max, AluOpType.mult).then_inc(act, 1)
-            g.vector.tensor_scalar(T.tl[:, 4 * a + 1:4 * b:4], za, -CONST, 0.0, AluOpType.mult, AluOpType.max).then_inc(act, 1)
-            g.scalar.wait_ge(S["zb%d" % j], 1)
-            g.scalar.activation(T.tl[:, 4 * a + 2:4 * b:4], zb, ActivationFunctionType.Relu, scale=CONST).then_inc(act, 1)
-            g.scalar.activation(T.tl[:, 4 * a + 3:4 * b:4], zb, ActivationFunctionType.Relu, scale=-CONST).then_inc(act, 1)
-            g.vector.wait_ge(act, 4)
-            g.vector.quantize_mx(T.outq[:, a:b], T.outs[:, a:b], T.tl[:, 4 * a:4 * b]).then_inc(S["qd%d" % j], 1)
-
-    dst = T.cores[(rank + 1) % N]
-    rid, pid = topo.addr(dst, core)
-    ec, es = engines(core, dst)
-    left = 0
-    for j, (a, b) in enumerate(out_plan):
-        g.wait_ge(S["qd%d" % j], 1)
-        g.remote_dma(T.inq[:, a:b].bitcast(dt.uint8), T.outq[:, a:b].bitcast(dt.uint8),
-                     S["arr%d" % j], S.sent, pid, rid, bits(ec))
-        g.remote_dma(T.ins[:, a:b], T.outs[:, a:b], S["arr%d" % j], S.sent, pid, rid, bits(es))
-        left += len(ec) + len(es)
-
-    if last:
-        stores = 0
-        for j, (a, b) in enumerate(comp_plan):
-            cuts = []
-            for m in range(a // TILE, (b + TILE - 1) // TILE):
-                cuts.append((m, max(a, m * TILE), min(b, (m + 1) * TILE)))
-            g.vector.wait_ge(S["za%d" % j], 1)
-            g.scalar.wait_ge(S["zb%d" % j], 1)
-            for i in range(2):
-                for (m, lo, hi) in cuts:
-                    k = 512 * (2 * j + i)
-                    z = T.ps[:, k + lo - a:k + hi - a]
-                    o = TILE * (2 * m + i) - m * TILE
-                    if i == 0:
-                        g.vector.tensor_copy(T.yb[:, o + lo:o + hi], z).then_inc(S["ca%d" % j], 1)
-                    else:
-                        g.scalar.activation(T.yb[:, o + lo:o + hi], z, ActivationFunctionType.Copy).then_inc(S["cb%d" % j], 1)
-            g.sync.wait_ge(S["ca%d" % j], len(cuts))
-            g.scalar.wait_ge(S["cb%d" % j], len(cuts))
-            for i, q in enumerate((g.sync, g.scalar)):
-                for (m, lo, hi) in cuts:
-                    o = TILE * (2 * m + i) - m * TILE
-                    q.dma_start(T.y[:, o + lo:o + hi], T.yb[:, o + lo:o + hi]).then_inc(S.stored, 16)
-                    stores += 1
-        g.wait_ge(S.stored, 16 * stores)
-
-    g.wait_ge(S.sent, left)
+    g.wait_ge(S.sent, left[0])

@@ -5,8 +5,11 @@ N = 8
 WORLD = 512
 COLS = 384
 TILE = 128
+NT = COLS // TILE
 HW = 192
 HALVES = [(0, HW), (HW, COLS)]
+PAIRCUT = [([(0, 96), (96, 192)], [(0, 192)]),
+           ([(192, 256), (256, 320), (320, 384)], [(192, 256), (256, 384)])]
 CONST = float(np.float32(0.023))
 
 SEQ = [[(0, (0,)), (1, (1, 2)), (4, (3, 4)), (5, (5, 6)), (N - 1, (N - 1,))],
@@ -21,23 +24,24 @@ SCRATCH = {
     "xt":  ("sbuf", [128, 4 * COLS], "bfloat16"),
     "xq":  ("sbuf", [128, COLS], "float8_e4m3fn_x4"),
     "xsc": ("sbuf", [128, COLS], "uint8"),
-    "tl":  ("sbuf", [128, 4 * 2 * HW], "bfloat16"),
-    "oq":  ("sbuf", [128, 2 * HW], "float8_e4m3fn_x4"),
-    "osc": ("sbuf", [128, 2 * HW], "uint8"),
+    "tl":  ("sbuf", [128, 4 * COLS], "bfloat16"),
+    "oq":  ("sbuf", [128, COLS], "float8_e4m3fn_x4"),
+    "osc": ("sbuf", [128, COLS], "uint8"),
     "inq": ("sbuf", [128, COLS], "float8_e4m3fn_x4"),
     "ins": ("sbuf", [128, COLS], "uint8"),
-    "ps":  ("psum", [128, 512 * 4], "float32"),
+    "ps":  ("psum", [128, 512 * 2 * NT], "float32"),
     "yb":  ("sbuf", [128, 2 * COLS], "float32"),
 }
 SEMAPHORES = (["wl", "wqd", "warr", "sent", "stored"]
-              + ["%s%d" % (n, j) for n in ("xl", "xqd", "arr", "za", "zb", "act", "qd", "ca", "cb") for j in range(2)])
+              + ["%s%d" % (n, j) for n in ("xl", "xqd", "xa", "arr", "pc", "za", "zb", "act", "qd", "ca", "cb")
+                 for j in range(NT)])
 
 _CACHE = {}
 
 
-def _roads(T, topo):
-    if "r" in _CACHE:
-        return _CACHE["r"]
+def _plan(T, topo):
+    if "p" in _CACHE:
+        return _CACHE["p"]
     cores = list(T.cores)
 
     def place(c):
@@ -49,140 +53,195 @@ def _roads(T, topo):
         return topo.same_plane(a, b)
 
     full = [[(cores[N - 1], "x")] + [(cores[r], st) for r, st in seq] for seq in SEQ]
-    roads = []
+    roads, pairs = [], []
     for h, seq in enumerate(full):
         other = full[1 - h]
-        road = [seq[0]]
+        road = [((seq[0][0], seq[0][0]), seq[0][1])]
         for k in range(1, len(seq)):
             a, b = seq[k - 1][0], seq[k][0]
             if not topo.may_write(a, b):
                 shun = (place(other[k - 1][0]), place(other[k][0]))
-                road.append(([c for c in range(WORLD) if c not in cores and topo.may_write(a, c) and topo.may_write(c, b)
-                              and one_link(a, c) and one_link(c, b) and topo.die(c) == topo.die(a)
-                              and place(c) not in shun][0], ()))
-            road.append(seq[k])
+                fit = [c for c in range(WORLD) if c not in cores and topo.may_write(a, c) and topo.may_write(c, b)
+                       and one_link(a, c) and one_link(c, b) and topo.die(c) == topo.die(a) and place(c) not in shun]
+                fit = [c for c in fit if place(c) == place(fit[0])]
+                pairs.append((fit[-2], fit[-1]))
+                road.append((pairs[-1], ()))
+            road.append(((b, b), seq[k][1]))
         roads.append(road)
-    _CACHE["r"] = roads
-    return roads
+    via = {}
+    for road in roads:
+        for (c, _), st in road:
+            for s in (st if st not in ("x", ()) else ()):
+                src = cores[s]
+                if src != c:
+                    for pr in pairs:
+                        if place(pr[0]) == place(src) and all(topo.may_write(src, p) and topo.may_write(p, c) for p in pr):
+                            via[(src, c)] = pr
+    _CACHE["p"] = (roads, via)
+    return _CACHE["p"]
 
 
 def rank_program(g, core, T, topo):
-    roads = _roads(T, topo)
-    jobs = [(h, k, st) for h, road in enumerate(roads) for k, (c, st) in enumerate(road) if c == core]
+    roads, via = _plan(T, topo)
+    jobs = [(h, k, st) for h, road in enumerate(roads) for k, (who, st) in enumerate(road) if core in who]
     if not jobs:
         return
     rank = T.rank_of(core)
     S = T.sem
-    last = rank == N - 1
     left = [0]
+    tiles = [(TILE * m, TILE * m + TILE) for m in range(NT)]
 
     def engines(src, dst):
         m = topo.mask(src, dst)
-        e = [i for i in range(m.bit_length()) if (m >> i) & 1]
-        return e[0::2], e[1::2]
+        return [i for i in range(m.bit_length()) if (m >> i) & 1]
 
-    def lands(src):
-        ec, es = engines(src, core)
-        return len(ec) + len(es)
+    def share(src, who, part, dst):
+        e = engines(src, dst)
+        return e[part::2] if who[0] == who[1] else e
 
-    def send(dst, dq, ds, sq, ss, sem):
+    def lands(who, parts=(0, 1)):
+        return sum(len(share(who[p], who, p, core)) for p in parts)
+
+    def put(part, who, dst, d, s, sem):
         rid, pid = topo.addr(dst, core)
-        ec, es = engines(core, dst)
-        g.remote_dma(dq.bitcast(dt.uint8), sq.bitcast(dt.uint8), sem, S.sent, pid, rid, sum(1 << i for i in ec))
-        g.remote_dma(ds, ss, sem, S.sent, pid, rid, sum(1 << i for i in es))
-        left[0] += len(ec) + len(es)
+        e = share(core, who, part, dst)
+        if part == 0:
+            d, s = d.bitcast(dt.uint8), s.bitcast(dt.uint8)
+        g.remote_dma(d, s, sem, S.sent, pid, rid, sum(1 << i for i in e))
+        left[0] += len(e)
 
-    if last:
-        for h, (a, b) in enumerate(HALVES):
-            (g.sync, g.scalar)[h].dma_start(T.xt[:, 4 * a:4 * b], T.x[:, 4 * a:4 * b]).then_inc(S["xl%d" % h], 16)
-    if rank is not None:
-        g.sync.dma_start(T.wt[:, :], T.w[:, :]).then_inc(S.wl, 16)
-    if last:
-        for h, (a, b) in enumerate(HALVES):
-            g.vector.wait_ge(S["xl%d" % h], 16)
-            g.vector.quantize_mx(T.xq[:, a:b], T.xsc[:, a:b], T.xt[:, 4 * a:4 * b]).then_inc(S["xqd%d" % h], 1)
-    if rank is not None:
+    def send(to, dq, ds, sq, ss, sem):
+        put(0, (core, core), to[0], dq, sq, sem)
+        put(1, (core, core), to[1], ds, ss, sem)
+
+    def pass_on(h, k, lo, hi, bq, bs, sh):
+        to = roads[h][k + 1][0]
+        me = (core, core)
+        if to[0] != to[1]:
+            calls = [(p, j, c0, c1) for p in (0, 1) for j, (c0, c1) in enumerate(PAIRCUT[h][p]) if lo <= c0 and c1 <= hi]
+            calls = calls[:1] + [c for c in calls if c[0] == 1] + [c for c in calls[1:] if c[0] == 0]
+            for (p, j, c0, c1) in calls:
+                put(p, me, to[p], (T.inq, T.ins)[p][:, c0:c1], (bq, bs)[p][:, c0 + sh:c1 + sh], S["pc%d" % j])
+        elif k + 2 == len(roads[h]) and lo // TILE != (hi - 1) // TILE:
+            cut = (lo // TILE + 1) * TILE
+            put(0, me, to[0], T.inq[:, lo:cut], bq[:, lo + sh:cut + sh], S["arr%d" % (lo // TILE)])
+            put(1, me, to[1], T.ins[:, lo:hi], bs[:, lo + sh:hi + sh], S["arr%d" % (lo // TILE)])
+            put(0, me, to[0], T.inq[:, cut:hi], bq[:, cut + sh:hi + sh], S["arr%d" % (cut // TILE)])
+        else:
+            send(to, T.inq[:, lo:hi], T.ins[:, lo:hi], bq[:, lo + sh:hi + sh], bs[:, lo + sh:hi + sh], S["arr%d" % h])
+
+    def from_pair(h, pr):
+        return sum(len(PAIRCUT[h][p]) * lands(pr, (p,)) for p in (0, 1))
+
+    def products(slot, n, wq, ws, cq, cs):
+        z = []
+        for i, nm in enumerate(("za", "zb")):
+            o = 512 * (2 * slot + i)
+            z.append(T.ps[:, o:o + n])
+            g.tensor.matmul_mx(z[i], wq[:, 128 * i:128 * i + 128], ws[:, 128 * i:128 * i + 128],
+                               cq, cs, True, True).then_inc(S["%s%d" % (nm, slot)], 1)
+        g.vector.wait_ge(S["za%d" % slot], 1)
+        g.scalar.wait_ge(S["zb%d" % slot], 1)
+        return z
+
+    def requant(slot, off, n, z):
+        lo, hi = 4 * off, 4 * (off + n)
+        act = S["act%d" % slot]
+        g.vector.tensor_scalar(T.tl[:, lo + 0:hi:4], z[0], 0.0, CONST, AluOpType.max, AluOpType.mult).then_inc(act, 1)
+        g.vector.tensor_scalar(T.tl[:, lo + 1:hi:4], z[0], -CONST, 0.0, AluOpType.mult, AluOpType.max).then_inc(act, 1)
+        g.scalar.activation(T.tl[:, lo + 2:hi:4], z[1], ActivationFunctionType.Relu, scale=CONST).then_inc(act, 1)
+        g.scalar.activation(T.tl[:, lo + 3:hi:4], z[1], ActivationFunctionType.Relu, scale=-CONST).then_inc(act, 1)
+        g.vector.wait_ge(act, 4)
+        g.vector.quantize_mx(T.oq[:, off:off + n], T.osc[:, off:off + n], T.tl[:, lo:hi]).then_inc(S["qd%d" % slot], 1)
+        return T.oq[:, off:off + n], T.osc[:, off:off + n]
+
+    if rank is None:
+        for (src, dst), pr in via.items():
+            if core in pr:
+                p = pr.index(core)
+                g.wait_ge(S.warr, lands((src, src), (p,)))
+                put(p, pr, dst, (T.fq, T.fsc)[p][:, :], (T.fq, T.fsc)[p][:, :], S.warr)
+        for (h, k, st) in jobs:
+            pr = roads[h][k][0]
+            p = pr.index(core)
+            n = lands(roads[h][k - 1][0], (p,))
+            for j, (c0, c1) in enumerate(PAIRCUT[h][p]):
+                g.wait_ge(S["pc%d" % j], n)
+                put(p, pr, roads[h][k + 1][0][p], (T.inq, T.ins)[p][:, c0:c1], (T.inq, T.ins)[p][:, c0:c1], S["arr%d" % h])
+        g.wait_ge(S.sent, left[0])
+        return
+
+    if rank == N - 1:
+        for m, (c0, c1) in enumerate(tiles):
+            (g.sync, g.scalar)[m % 2].dma_start(T.xt[:, 4 * c0:4 * c1], T.x[:, 4 * c0:4 * c1]).then_inc(S["xl%d" % m], 16)
+        g.scalar.dma_start(T.wt[:, :], T.w[:, :]).then_inc(S.wl, 16)
+        for m, (c0, c1) in enumerate(tiles):
+            g.vector.wait_ge(S["xl%d" % m], 16)
+            g.vector.quantize_mx(T.xq[:, c0:c1], T.xsc[:, c0:c1], T.xt[:, 4 * c0:4 * c1]).then_inc(S["xqd%d" % m], 1)
         g.vector.wait_ge(S.wl, 16)
         g.vector.quantize_mx(T.wq[:, :], T.wsc[:, :], T.wt[:, :]).then_inc(S.wqd, 1)
-        takers = [c for road in roads for (c, st) in road if st != "x" and rank in st and c != core]
-        if takers:
-            g.wait_ge(S.wqd, 1)
-        for c in takers:
-            send(c, T.fq[:, :], T.fsc[:, :], T.wq[:, :], T.wsc[:, :], S.warr)
+        for m, (c0, c1) in enumerate(tiles):
+            g.wait_ge(S["xqd%d" % m], 1)
+            send(roads[0][1][0], T.inq[:, c0:c1], T.ins[:, c0:c1], T.xq[:, c0:c1], T.xsc[:, c0:c1], S["xa%d" % m])
+        g.tensor.wait_ge(S.wqd, 1)
+        p0, p1 = roads[0][-2][0], roads[1][-2][0]
+        need = [from_pair(0, p0), lands(p1), lands(p1, (0,))]
+        for m, (c0, c1) in enumerate(tiles):
+            g.tensor.wait_ge(S["arr%d" % m], need[m])
+            z = products(m, TILE, T.wq, T.wsc, T.inq[:, c0:c1], T.ins[:, c0:c1])
+            g.vector.tensor_copy(T.yb[:, 2 * c0:2 * c0 + TILE], z[0]).then_inc(S["ca%d" % m], 1)
+            g.scalar.activation(T.yb[:, 2 * c0 + TILE:2 * c1], z[1], ActivationFunctionType.Copy).then_inc(S["cb%d" % m], 1)
+            g.sync.wait_ge(S["ca%d" % m], 1)
+            g.sync.wait_ge(S["cb%d" % m], 1)
+            g.sync.dma_start(T.y[:, 2 * c0:2 * c1], T.yb[:, 2 * c0:2 * c1]).then_inc(S.stored, 16)
+        g.wait_ge(S.stored, 16 * NT)
+        g.wait_ge(S.sent, left[0])
+        return
 
-    slot = 0
-    ready = set()
-    ycols = []
-    for (h, k, st) in jobs:
-        a, b = HALVES[h]
-        road = roads[h]
-        arr = S["arr%d" % h]
-        if st == "x":
-            g.wait_ge(S["xqd%d" % h], 1)
-            send(road[k + 1][0], T.inq[:, a:b], T.ins[:, a:b], T.xq[:, a:b], T.xsc[:, a:b], arr)
-            continue
-        if st == ():
-            g.wait_ge(arr, lands(road[k - 1][0]))
-            send(road[k + 1][0], T.inq[:, a:b], T.ins[:, a:b], T.inq[:, a:b], T.ins[:, a:b], arr)
-            continue
-        cq, cs = T.inq[:, a:b], T.ins[:, a:b]
-        for t, s in enumerate(st):
-            if s == rank:
-                wq, ws, wsem, wn = T.wq, T.wsc, S.wqd, 1
-            else:
-                wq, ws, wsem, wn = T.fq, T.fsc, S.warr, lands(T.cores[s])
-            if s not in ready:
-                g.tensor.wait_ge(wsem, wn)
-                ready.add(s)
-            if t == 0:
-                g.tensor.wait_ge(arr, lands(road[k - 1][0]))
-            else:
-                g.tensor.wait_ge(S["qd%d" % (slot - 1)], 1)
-            z = []
-            for i, nm in enumerate(("za", "zb")):
-                o = 512 * (2 * slot + i)
-                z.append(T.ps[:, o:o + HW])
-                g.tensor.matmul_mx(z[i], wq[:, 128 * i:128 * i + 128], ws[:, 128 * i:128 * i + 128],
-                                   cq, cs, True, True).then_inc(S["%s%d" % (nm, slot)], 1)
-            g.vector.wait_ge(S["za%d" % slot], 1)
-            g.scalar.wait_ge(S["zb%d" % slot], 1)
-            if s < N - 1:
-                lo, hi = 4 * HW * slot, 4 * HW * (slot + 1)
-                act = S["act%d" % slot]
-                g.vector.tensor_scalar(T.tl[:, lo + 0:hi:4], z[0], 0.0, CONST, AluOpType.max, AluOpType.mult).then_inc(act, 1)
-                g.vector.tensor_scalar(T.tl[:, lo + 1:hi:4], z[0], -CONST, 0.0, AluOpType.mult, AluOpType.max).then_inc(act, 1)
-                g.scalar.activation(T.tl[:, lo + 2:hi:4], z[1], ActivationFunctionType.Relu, scale=CONST).then_inc(act, 1)
-                g.scalar.activation(T.tl[:, lo + 3:hi:4], z[1], ActivationFunctionType.Relu, scale=-CONST).then_inc(act, 1)
-                cq, cs = T.oq[:, HW * slot:HW * (slot + 1)], T.osc[:, HW * slot:HW * (slot + 1)]
-                g.vector.wait_ge(act, 4)
-                g.vector.quantize_mx(cq, cs, T.tl[:, lo:hi]).then_inc(S["qd%d" % slot], 1)
-            else:
-                filled = set()
-                for m in range(a // TILE, (b + TILE - 1) // TILE):
-                    lo, hi = max(a, m * TILE), min(b, (m + 1) * TILE)
-                    for i in range(2):
-                        o = TILE * (2 * m + i) - m * TILE
-                        zz = T.ps[:, 512 * (2 * slot + i) + lo - a:512 * (2 * slot + i) + hi - a]
-                        if i == 0:
-                            g.vector.tensor_copy(T.yb[:, o + lo:o + hi], zz).then_inc(S["ca%d" % h], 1)
-                        else:
-                            g.scalar.activation(T.yb[:, o + lo:o + hi], zz, ActivationFunctionType.Copy).then_inc(S["cb%d" % h], 1)
-                        filled.update(range(o + lo, o + hi))
-                ycols.append((h, filled, (b + TILE - 1) // TILE - a // TILE))
-            slot += 1
-        if k + 1 < len(road):
-            g.wait_ge(S["qd%d" % (slot - 1)], 1)
-            send(road[k + 1][0], T.inq[:, a:b], T.ins[:, a:b], cq, cs, arr)
+    g.sync.dma_start(T.wt[:, :], T.w[:, :]).then_inc(S.wl, 16)
+    g.vector.wait_ge(S.wl, 16)
+    g.vector.quantize_mx(T.wq[:, :], T.wsc[:, :], T.wt[:, :]).then_inc(S.wqd, 1)
 
-    if last:
-        cut = 0
-        while cut in ycols[0][1]:
-            cut += 1
-        for j, (lo, hi) in enumerate(((0, cut), (cut, 2 * COLS))):
-            h, _, n = ycols[j]
-            g.sync.wait_ge(S["ca%d" % h], n)
-            g.sync.wait_ge(S["cb%d" % h], n)
-            g.sync.dma_start(T.y[:, lo:hi], T.yb[:, lo:hi]).then_inc(S.stored, 16)
-        g.wait_ge(S.stored, 32)
+    if len(jobs) > 1:
+        g.tensor.wait_ge(S.wqd, 1)
+        for m, (c0, c1) in enumerate(tiles):
+            g.tensor.wait_ge(S["xa%d" % m], lands(roads[0][0][0]))
+            requant(m, c0, TILE, products(m, TILE, T.wq, T.wsc, T.inq[:, c0:c1], T.ins[:, c0:c1]))
+            g.wait_ge(S["qd%d" % m], 1)
+            for (h, k, st) in jobs:
+                lo, hi = max(c0, HALVES[h][0]), min(c1, HALVES[h][1])
+                if lo < hi:
+                    pass_on(h, k, lo, hi, T.oq, T.osc, 0)
+        g.wait_ge(S.sent, left[0])
+        return
 
+    (h, k, st), = jobs
+    a, b = HALVES[h]
+    road = roads[h]
+    g.wait_ge(S.wqd, 1)
+    for c in [who[0] for rd in roads for (who, s2) in rd if s2 != "x" and rank in s2 and who[0] != core]:
+        send(via.get((core, c), (c, c)), T.fq[:, :], T.fsc[:, :], T.wq[:, :], T.wsc[:, :], S.warr)
+    prev = road[k - 1][0]
+    if prev[0] != prev[1]:
+        n_in = from_pair(h, prev)
+    elif k == 2:
+        n_in = lands(prev) * len([1 for (c0, c1) in tiles if max(c0, a) < min(c1, b)])
+    else:
+        n_in = lands(prev)
+    cq, cs = T.inq[:, a:b], T.ins[:, a:b]
+    for t, s in enumerate(st):
+        if s == rank:
+            wq, ws = T.wq, T.wsc
+            g.tensor.wait_ge(S.wqd, 1)
+        else:
+            src = T.cores[s]
+            wq, ws = T.fq, T.fsc
+            g.tensor.wait_ge(S.warr, lands(via.get((src, core), (src, src))))
+        if t == 0:
+            g.tensor.wait_ge(S["arr%d" % h], n_in)
+        else:
+            g.tensor.wait_ge(S["qd%d" % (t - 1)], 1)
+        cq, cs = requant(t, HW * t, HW, products(t, HW, wq, ws, cq, cs))
+    g.wait_ge(S["qd%d" % (len(st) - 1)], 1)
+    pass_on(h, k, a, b, T.oq, T.osc, HW * (len(st) - 1) - a)
     g.wait_ge(S.sent, left[0])

import numpy as np
from concourse.mybir import dt, AluOpType, ActivationFunctionType

N = 8
WORLD = 512
COLS = 384
TILE = 128
NT = COLS // TILE
HW = 192
HALVES = [(0, HW), (HW, COLS)]
PAIRCUT = [([(0, 96), (96, 192)], [(0, 192)]),
           ([(192, 256), (256, 320), (320, 384)], [(192, 256), (256, 384)])]
CONST = float(np.float32(0.023))

SEQ = [[(0, (0,)), (1, (1, 2)), (4, (3, 4)), (5, (5, 6)), (N - 1, (N - 1,))],
       [(0, (0,)), (2, (1, 2)), (3, (3, 4)), (6, (5, 6)), (N - 1, (N - 1,))]]

SCRATCH = {
    "wt":  ("sbuf", [128, 1024], "bfloat16"),
    "wq":  ("sbuf", [128, 256], "float8_e4m3fn_x4"),
    "wsc": ("sbuf", [128, 256], "uint8"),
    "fq":  ("sbuf", [128, 256], "float8_e4m3fn_x4"),
    "fsc": ("sbuf", [128, 256], "uint8"),
    "xt":  ("sbuf", [128, 4 * COLS], "bfloat16"),
    "xq":  ("sbuf", [128, COLS], "float8_e4m3fn_x4"),
    "xsc": ("sbuf", [128, COLS], "uint8"),
    "tl":  ("sbuf", [128, 4 * COLS], "bfloat16"),
    "oq":  ("sbuf", [128, COLS], "float8_e4m3fn_x4"),
    "osc": ("sbuf", [128, COLS], "uint8"),
    "inq": ("sbuf", [128, COLS], "float8_e4m3fn_x4"),
    "ins": ("sbuf", [128, COLS], "uint8"),
    "ps":  ("psum", [128, 512 * 2 * NT], "float32"),
    "yb":  ("sbuf", [128, 2 * COLS], "float32"),
}
SEMAPHORES = (["wl", "wqd", "warr", "sent", "stored"]
              + ["%s%d" % (n, j) for n in ("xl", "xqd", "xa", "arr", "pc", "za", "zb", "act", "qd", "ca", "cb")
                 for j in range(NT)])

_CACHE = {}


def _plan(T, topo):
    if "p" in _CACHE:
        return _CACHE["p"]
    cores = list(T.cores)

    def place(c):
        return (topo.host(c), topo.chip(c))

    def one_link(a, b):
        if topo.rack(topo.host(a)) != topo.rack(topo.host(b)):
            return topo.chip(a) == topo.chip(b)
        return topo.same_plane(a, b)

    full = [[(cores[N - 1], "x")] + [(cores[r], st) for r, st in seq] for seq in SEQ]
    roads, pairs = [], []
    for h, seq in enumerate(full):
        other = full[1 - h]
        road = [((seq[0][0], seq[0][0]), seq[0][1])]
        for k in range(1, len(seq)):
            a, b = seq[k - 1][0], seq[k][0]
            if not topo.may_write(a, b):
                shun = (place(other[k - 1][0]), place(other[k][0]))
                fit = [c for c in range(WORLD) if c not in cores and topo.may_write(a, c) and topo.may_write(c, b)
                       and one_link(a, c) and one_link(c, b) and topo.die(c) == topo.die(a) and place(c) not in shun]
                fit = [c for c in fit if place(c) == place(fit[0])]
                pairs.append((fit[-2], fit[-1]))
                road.append((pairs[-1], ()))
            road.append(((b, b), seq[k][1]))
        roads.append(road)
    via = {}
    for road in roads:
        for (c, _), st in road:
            for s in (st if st not in ("x", ()) else ()):
                src = cores[s]
                if src != c:
                    for pr in pairs:
                        if place(pr[0]) == place(src) and all(topo.may_write(src, p) and topo.may_write(p, c) for p in pr):
                            via[(src, c)] = pr
    _CACHE["p"] = (roads, via)
    return _CACHE["p"]


def rank_program(g, core, T, topo):
    roads, via = _plan(T, topo)
    jobs = [(h, k, st) for h, road in enumerate(roads) for k, (who, st) in enumerate(road) if core in who]
    if not jobs:
        return
    rank = T.rank_of(core)
    S = T.sem
    left = [0]
    tiles = [(TILE * m, TILE * m + TILE) for m in range(NT)]

    def engines(src, dst):
        m = topo.mask(src, dst)
        return [i for i in range(m.bit_length()) if (m >> i) & 1]

    def share(src, who, part, dst):
        e = engines(src, dst)
        return e[part::2] if who[0] == who[1] else e

    def lands(who, parts=(0, 1)):
        return sum(len(share(who[p], who, p, core)) for p in parts)

    def put(part, who, dst, d, s, sem):
        rid, pid = topo.addr(dst, core)
        e = share(core, who, part, dst)
        if part == 0:
            d, s = d.bitcast(dt.uint8), s.bitcast(dt.uint8)
        g.remote_dma(d, s, sem, S.sent, pid, rid, sum(1 << i for i in e))
        left[0] += len(e)

    def send(to, dq, ds, sq, ss, sem):
        put(0, (core, core), to[0], dq, sq, sem)
        put(1, (core, core), to[1], ds, ss, sem)

    def pass_on(h, k, lo, hi, bq, bs, sh):
        to = roads[h][k + 1][0]
        me = (core, core)
        if to[0] != to[1]:
            calls = [(p, j, c0, c1) for p in (0, 1) for j, (c0, c1) in enumerate(PAIRCUT[h][p]) if lo <= c0 and c1 <= hi]
            calls = calls[:1] + [c for c in calls if c[0] == 1] + [c for c in calls[1:] if c[0] == 0]
            for (p, j, c0, c1) in calls:
                put(p, me, to[p], (T.inq, T.ins)[p][:, c0:c1], (bq, bs)[p][:, c0 + sh:c1 + sh], S["pc%d" % j])
        elif k + 2 == len(roads[h]) and lo // TILE != (hi - 1) // TILE:
            cut = (lo // TILE + 1) * TILE
            put(0, me, to[0], T.inq[:, lo:cut], bq[:, lo + sh:cut + sh], S["arr%d" % (lo // TILE)])
            put(1, me, to[1], T.ins[:, lo:hi], bs[:, lo + sh:hi + sh], S["arr%d" % (lo // TILE)])
            put(0, me, to[0], T.inq[:, cut:hi], bq[:, cut + sh:hi + sh], S["arr%d" % (cut // TILE)])
        else:
            send(to, T.inq[:, lo:hi], T.ins[:, lo:hi], bq[:, lo + sh:hi + sh], bs[:, lo + sh:hi + sh], S["arr%d" % h])

    def from_pair(h, pr):
        return sum(len(PAIRCUT[h][p]) * lands(pr, (p,)) for p in (0, 1))

    def products(slot, n, wq, ws, cq, cs):
        z = []
        for i, nm in enumerate(("za", "zb")):
            o = 512 * (2 * slot + i)
            z.append(T.ps[:, o:o + n])
            g.tensor.matmul_mx(z[i], wq[:, 128 * i:128 * i + 128], ws[:, 128 * i:128 * i + 128],
                               cq, cs, True, True).then_inc(S["%s%d" % (nm, slot)], 1)
        g.vector.wait_ge(S["za%d" % slot], 1)
        g.scalar.wait_ge(S["zb%d" % slot], 1)
        return z

    def requant(slot, off, n, z):
        lo, hi = 4 * off, 4 * (off + n)
        act = S["act%d" % slot]
        g.vector.tensor_scalar(T.tl[:, lo + 0:hi:4], z[0], 0.0, CONST, AluOpType.max, AluOpType.mult).then_inc(act, 1)
        g.vector.tensor_scalar(T.tl[:, lo + 1:hi:4], z[0], -CONST, 0.0, AluOpType.mult, AluOpType.max).then_inc(act, 1)
        g.scalar.activation(T.tl[:, lo + 2:hi:4], z[1], ActivationFunctionType.Relu, scale=CONST).then_inc(act, 1)
        g.scalar.activation(T.tl[:, lo + 3:hi:4], z[1], ActivationFunctionType.Relu, scale=-CONST).then_inc(act, 1)
        g.vector.wait_ge(act, 4)
        g.vector.quantize_mx(T.oq[:, off:off + n], T.osc[:, off:off + n], T.tl[:, lo:hi]).then_inc(S["qd%d" % slot], 1)
        return T.oq[:, off:off + n], T.osc[:, off:off + n]

    if rank is None:
        for (src, dst), pr in via.items():
            if core in pr:
                p = pr.index(core)
                g.wait_ge(S.warr, lands((src, src), (p,)))
                put(p, pr, dst, (T.fq, T.fsc)[p][:, :], (T.fq, T.fsc)[p][:, :], S.warr)
        for (h, k, st) in jobs:
            pr = roads[h][k][0]
            p = pr.index(core)
            n = lands(roads[h][k - 1][0], (p,))
            for j, (c0, c1) in enumerate(PAIRCUT[h][p]):
                g.wait_ge(S["pc%d" % j], n)
                put(p, pr, roads[h][k + 1][0][p], (T.inq, T.ins)[p][:, c0:c1], (T.inq, T.ins)[p][:, c0:c1], S["arr%d" % h])
        g.wait_ge(S.sent, left[0])
        return

    if rank == N - 1:
        for m, (c0, c1) in enumerate(tiles):
            (g.sync, g.scalar)[m % 2].dma_start(T.xt[:, 4 * c0:4 * c1], T.x[:, 4 * c0:4 * c1]).then_inc(S["xl%d" % m], 16)
        g.scalar.dma_start(T.wt[:, :], T.w[:, :]).then_inc(S.wl, 16)
        for m, (c0, c1) in enumerate(tiles):
            g.vector.wait_ge(S["xl%d" % m], 16)
            g.vector.quantize_mx(T.xq[:, c0:c1], T.xsc[:, c0:c1], T.xt[:, 4 * c0:4 * c1]).then_inc(S["xqd%d" % m], 1)
        g.vector.wait_ge(S.wl, 16)
        g.vector.quantize_mx(T.wq[:, :], T.wsc[:, :], T.wt[:, :]).then_inc(S.wqd, 1)
        for m, (c0, c1) in enumerate(tiles):
            g.wait_ge(S["xqd%d" % m], 1)
            send(roads[0][1][0], T.inq[:, c0:c1], T.ins[:, c0:c1], T.xq[:, c0:c1], T.xsc[:, c0:c1], S["xa%d" % m])
        g.tensor.wait_ge(S.wqd, 1)
        p0, p1 = roads[0][-2][0], roads[1][-2][0]
        need = [from_pair(0, p0), lands(p1), lands(p1, (0,))]
        for m, (c0, c1) in enumerate(tiles):
            g.tensor.wait_ge(S["arr%d" % m], need[m])
            z = products(m, TILE, T.wq, T.wsc, T.inq[:, c0:c1], T.ins[:, c0:c1])
            g.vector.tensor_copy(T.yb[:, 2 * c0:2 * c0 + TILE], z[0]).then_inc(S["ca%d" % m], 1)
            g.scalar.activation(T.yb[:, 2 * c0 + TILE:2 * c1], z[1], ActivationFunctionType.Copy).then_inc(S["cb%d" % m], 1)
            g.sync.wait_ge(S["ca%d" % m], 1)
            g.sync.wait_ge(S["cb%d" % m], 1)
            g.sync.dma_start(T.y[:, 2 * c0:2 * c1], T.yb[:, 2 * c0:2 * c1]).then_inc(S.stored, 16)
        g.wait_ge(S.stored, 16 * NT)
        g.wait_ge(S.sent, left[0])
        return

    g.sync.dma_start(T.wt[:, :], T.w[:, :]).then_inc(S.wl, 16)
    g.vector.wait_ge(S.wl, 16)
    g.vector.quantize_mx(T.wq[:, :], T.wsc[:, :], T.wt[:, :]).then_inc(S.wqd, 1)

    if len(jobs) > 1:
        g.tensor.wait_ge(S.wqd, 1)
        for m, (c0, c1) in enumerate(tiles):
            g.tensor.wait_ge(S["xa%d" % m], lands(roads[0][0][0]))
            requant(m, c0, TILE, products(m, TILE, T.wq, T.wsc, T.inq[:, c0:c1], T.ins[:, c0:c1]))
            g.wait_ge(S["qd%d" % m], 1)
            for (h, k, st) in jobs:
                lo, hi = max(c0, HALVES[h][0]), min(c1, HALVES[h][1])
                if lo < hi:
                    pass_on(h, k, lo, hi, T.oq, T.osc, 0)
        g.wait_ge(S.sent, left[0])
        return

    (h, k, st), = jobs
    a, b = HALVES[h]
    road = roads[h]
    g.wait_ge(S.wqd, 1)
    for c in [who[0] for rd in roads for (who, s2) in rd if s2 != "x" and rank in s2 and who[0] != core]:
        send(via.get((core, c), (c, c)), T.fq[:, :], T.fsc[:, :], T.wq[:, :], T.wsc[:, :], S.warr)
    prev = road[k - 1][0]
    if prev[0] != prev[1]:
        n_in = from_pair(h, prev)
    elif k == 2:
        n_in = lands(prev) * len([1 for (c0, c1) in tiles if max(c0, a) < min(c1, b)])
    else:
        n_in = lands(prev)
    cq, cs = T.inq[:, a:b], T.ins[:, a:b]
    for t, s in enumerate(st):
        if s == rank:
            wq, ws = T.wq, T.wsc
            g.tensor.wait_ge(S.wqd, 1)
        else:
            src = T.cores[s]
            wq, ws = T.fq, T.fsc
            g.tensor.wait_ge(S.warr, lands(via.get((src, core), (src, src))))
        if t == 0:
            g.tensor.wait_ge(S["arr%d" % h], n_in)
        else:
            g.tensor.wait_ge(S["qd%d" % (t - 1)], 1)
        cq, cs = requant(t, HW * t, HW, products(t, HW, wq, ws, cq, cs))
    g.wait_ge(S["qd%d" % (len(st) - 1)], 1)
    pass_on(h, k, a, b, T.oq, T.osc, HW * (len(st) - 1) - a)
    g.wait_ge(S.sent, left[0])
